import numpy as np
import ml_dtypes


def mxq(x, axis, fmt="e4m3"):
    dtype, down = {"e4m3": (ml_dtypes.float8_e4m3fn, 7), "e5m2": (ml_dtypes.float8_e5m2, 14)}[fmt]
    v = np.moveaxis(np.asarray(x, np.float32).astype(ml_dtypes.bfloat16).astype(np.float64), axis, -1)
    blocks = v.reshape(v.shape[:-1] + (-1, 32))
    amax = np.abs(blocks).max(-1, keepdims=True)
    byte = np.maximum(np.where(amax > 0, np.frexp(amax)[1] - 1 + 127, 0) - down, 1)
    scale = np.exp2(byte - 127.0)
    codes = (blocks / scale).astype(np.float32).astype(dtype).astype(np.float64)
    return np.moveaxis((codes * scale).reshape(v.shape), -1, axis)


WIDE = False


def mx_kscale(k):
    if not WIDE:
        return np.ones(k)
    levels = np.array([10, -10, 5, -5, 0])
    if k % 512:
        return np.exp2(np.random.permutation(np.resize(levels, k // 32))).repeat(32)
    a = np.empty((k // 512, 16))
    for p in range(k // 512):
        a[p, :8] = np.random.permutation(np.resize(levels, 8))
        for g in range(8):
            far = levels[np.abs(levels - a[p, g]) >= 10]
            a[p, g + 8] = far[np.random.randint(len(far))]
    return np.exp2(a.ravel()).repeat(32)


def f64(x):
    return np.asarray(x).astype(np.float64)


def striped(idx):
    return np.tile(idx.reshape(-1, 16).T, (8, 1)).astype(np.uint16)


def unstriped(offs):
    return offs[:16].T.reshape(-1).astype(np.int64)


E2M1 = np.array([0.0, 0.5, 1.0, 1.5, 2.0, 3.0, 4.0, 6.0, -0.0, -0.5, -1.0, -1.5, -2.0, -3.0, -4.0, -6.0])


def pack_weight(w, fmt):
    k, n = w.shape
    w = f64(np.asarray(w, np.float32).astype(ml_dtypes.bfloat16)).reshape(k // 32, 32, n)
    amax = np.abs(w).max(1)
    if fmt == "e4m3":
        byte = np.frexp(amax)[1] - 1 + 127 - 7
    else:
        mant, ex = np.frexp(amax / 6.0)
        byte = np.where(mant > 0.5, ex, ex - 1) + 127
    byte = np.clip(np.where(amax > 0, byte, 1), 1, 254)
    scaled = (w * np.exp2(127.0 - byte)[:, None, :]).reshape(k, n).astype(np.float32)
    by_word = np.ascontiguousarray(scaled.reshape(k // 512, 128, 4, n).transpose(0, 1, 3, 2))
    if fmt == "e4m3":
        words = by_word.astype(ml_dtypes.float8_e4m3fn).view(np.uint8)
    else:
        c = by_word.astype(ml_dtypes.float4_e2m1fn).view(np.uint8) & 0xF
        words = (c[..., 0::2] | (c[..., 1::2] << 4)).reshape(k // 512, 128, 2 * n)
    return np.ascontiguousarray(words), np.ascontiguousarray(byte.astype(np.uint8).reshape(k // 512, 16, n))


def unpack_weight(words, scales, fmt):
    g, _, n = scales.shape
    words = np.ascontiguousarray(words).reshape(g, 128, n, -1)
    if fmt == "e4m3":
        vals = words.view(ml_dtypes.float8_e4m3fn).astype(np.float64)
    else:
        nib = np.empty((g, 128, n, 4), np.uint8)
        nib[..., 0::2] = words & 0xF
        nib[..., 1::2] = words >> 4
        vals = E2M1[nib]
    vals = vals * np.repeat(np.exp2(scales.astype(np.float64) - 127.0), 8, axis=1)[..., None]
    return vals.transpose(0, 1, 3, 2).reshape(g * 512, n)


def gelu(v):
    return 0.5 * v * (1.0 + np.tanh(np.sqrt(2.0 / np.pi) * (v + 0.044715 * v**3)))


def bf(x):
    return np.asarray(x, np.float32).astype(ml_dtypes.bfloat16)


def planes(Y):
    n, m = Y.shape
    b = f64(bf(Y)).reshape(n // 32, 32, m)
    amax = np.abs(b).max(1)
    byte = np.clip(np.where(amax > 0, np.frexp(amax)[1] - 1 + 127 - 7, 1), 1, 254)
    codes = (b * np.exp2(127.0 - byte)[:, None, :]).reshape(n, m).astype(np.float32).astype(ml_dtypes.float8_e4m3fn).view(np.uint8)
    words = codes.reshape(n // 512, 128, 4, m).transpose(0, 1, 3, 2)
    return np.ascontiguousarray(words), np.ascontiguousarray(byte.astype(np.uint8).reshape(n // 512, 16, m))


K, T, S, H, N, P = 1024, 4096, 1024, 512, 1024, 512


def setup_inputs():
    n = np.random.standard_normal
    s = mx_kscale(K)[:, None]
    u = mx_kscale(H)[:, None]
    ex = np.exp(0.8 * n(N))
    col = np.sqrt(ex)[None, :]
    d = {}
    d["tab_words"], d["tab_scales"] = pack_weight(n((K, T)) * s, "e4m3")
    d["offs"] = striped(np.random.permutation(T)[:S])
    d["w1"] = (n((K, H)) / s / K ** 0.5 * np.exp(0.4 * n((1, H)))).astype(np.float32)
    d["w2_words"], d["w2_scales"] = pack_weight(n((K, H)) / s / K ** 0.5, "e2m1")
    d["gain"] = (np.exp(0.3 * n(H)) * u[:, 0]).astype(np.float32)
    d["w3_words"], d["w3_scales"] = pack_weight(0.9 * n((H, N)) / u / H ** 0.5 * col, "e4m3")
    d["w4"] = (0.6 * n((K, N)) / s / K ** 0.5 * col).astype(np.float32)
    d["pos1"] = striped(np.random.permutation(S)[:P])
    d["pos2"] = striped(np.random.permutation(S)[:P])
    d["base"] = (0.8 * n((N, P)) * ex[:, None]).astype(np.float32)
    return d


def reference(tab_words, tab_scales, offs, w1, w2_words, w2_scales, gain, w3_words, w3_scales, w4, pos1, pos2, base):
    v = unpack_weight(tab_words, tab_scales, "e4m3")[:, unstriped(offs)]
    width = mxq(f64(w1), 0, "e4m3").T @ v
    trend = unpack_weight(w2_words, w2_scales, "e2m1").T @ v
    h = np.sqrt(np.abs(width)) * trend * f64(gain)[:, None]
    w3 = unpack_weight(w3_words, w3_scales, "e4m3")
    feat = w3.T @ mxq(h, 0, "e4m3") + mxq(f64(w4), 0, "e4m3").T @ v
    y = feat[:, unstriped(pos1)] * feat[:, unstriped(pos2)] + f64(base)
    words, scales = planes(y)
    return y, words, scales

@@ -1,0 +1,305 @@
+from contextlib import ExitStack
+
+import concourse.mybir as mybir
+
+K, T, S, H, N, M = 1024, 4096, 1024, 512, 1024, 512
+FLOPS = 5368709120
+
+F32 = mybir.dt.float32
+BF16 = mybir.dt.bfloat16
+I32 = mybir.dt.int32
+U32 = mybir.dt.uint32
+U16 = mybir.dt.uint16
+U8 = mybir.dt.uint8
+FP8X4 = mybir.dt.float8_e4m3fn_x4
+FP4X4 = mybir.dt.float4_e2m1fn_x4
+ACT = mybir.ActivationFunctionType
+MULT = mybir.AluOpType.mult
+ADD = mybir.AluOpType.add
+
+P = 128
+BANK = 512
+H_CHUNKS = [(0, 256), (256, 256), (512, 256), (768, 128), (896, 128)]
+W2_COL = S
+W3_COL = S + H
+
+
+def tile_list_ring_window_pairs_kernel(tc, tab_words, tab_scales, offs, w1, w2_words, w2_scales, gain,
+                                                 w3_words, w3_scales, w4, pos1, pos2, base, out_0, out_1, out_2):
+    nc = tc.nc
+    with ExitStack() as ctx:
+        lists = ctx.enter_context(tc.tile_pool(name="lists", bufs=1))
+        keep = ctx.enter_context(tc.tile_pool(name="keep", bufs=1))
+        ring = ctx.enter_context(tc.tile_pool(name="ring", bufs=3))
+        psum = ctx.enter_context(tc.psum_pool(name="psum", bufs=1))
+
+        def sb(name, shape, dtype, tag=None):
+            return keep.tile(shape, dtype, name=name, tag=tag or name, align_bytes=64)
+
+        def bank(i, name):
+            return psum.tile([P, BANK], F32, name=name, tag="bank%d" % i)
+
+        idx = lists.tile([P, S // 16], U16, name="idx")
+        nc.sync.dma_start(idx[:], offs)
+        scale_win = sb("scale_win", [P, T], U8)
+        nc.scalar.dma_start(scale_win[0:32, :].bitcast(I32), tab_scales.rearrange("a q t -> (a q) t").bitcast(I32))
+        w2s_raw = sb("w2s_raw", [P, H], U8)
+        nc.scalar.dma_start(w2s_raw[0:32, :].bitcast(I32), w2_scales.rearrange("a q c -> (a q) c").bitcast(I32))
+        nc.vector.memset(w2s_raw[32:64, :].bitcast(I32), 0)
+        nc.vector.memset(w2s_raw[64:128, :].bitcast(I32), 0)
+        w3s_raw = sb("w3s_raw", [P, N], U8)
+        nc.vector.memset(w3s_raw[:].bitcast(I32), 0)
+        warm = sb("warm", [P, 2], F32)
+        nc.vector.memset(warm[:], 1.0)
+        nc.vector.memset(scale_win[32:64, :].bitcast(I32), 0)
+        nc.vector.memset(scale_win[64:128, :].bitcast(I32), 0)
+        tab = []
+        for a in range(2):
+            tab.append(sb("tab%d" % a, [P, T], I32, tag="big%d" % a))
+            nc.sync.dma_start(tab[a][:], tab_words[a].rearrange("p n i -> p (n i)").bitcast(I32))
+        w2_raw = sb("w2_raw", [P, 2, 2 * H], U8)
+        nc.scalar.dma_start(w2_raw[:].bitcast(I32), w2_words.rearrange("a p c -> p a c").bitcast(I32))
+        gains = sb("gains", [P, 4], F32)
+        nc.scalar.dma_start(gains[:], gain.rearrange("(p t) -> p t", t=4))
+        nc.scalar.dma_start(w3s_raw[0:16, :].bitcast(I32), w3_scales[0].bitcast(I32))
+        nc.scalar.activation(warm[:, 1:2], warm[:, 0:1], ACT.Sqrt)
+        w1_raw = [sb("w1_raw%d" % a, [P, 4, H], F32, tag="mid%d" % a) for a in range(2)]
+        w1_rows = w1.rearrange("(a p j) c -> a p j c", a=2, j=4)
+        nc.sync.dma_start(w1_raw[0][:], w1_rows[0])
+        for c in range(2):
+            nc.sync.dma_start(w1_raw[1][:, :, 256 * c:256 * (c + 1)], w1_rows[1][:, :, 256 * c:256 * (c + 1)])
+        p1 = lists.tile([P, M // 16], U16, name="p1")
+        nc.sync.dma_start(p1[:], pos1)
+        p2 = lists.tile([P, M // 16], U16, name="p2")
+        nc.sync.dma_start(p2[:], pos2)
+        w4_rows = w4.rearrange("(a p j) c -> a p j c", a=2, j=4)
+        w4_raw = {}
+
+        def w4_load(g, a, tag):
+            w4_raw[g, a] = sb("w4_raw%d%d" % (g, a), [P, 4, BANK], F32, tag=tag)
+            nc.sync.dma_start(w4_raw[g, a][:], w4_rows[a][:, :, BANK * g:BANK * (g + 1)])
+
+        w4_load(0, 0, None)
+        w4_load(0, 1, None)
+        w3_raw = sb("w3_raw", [P, N], I32)
+        nc.sync.dma_start(w3_raw[:], w3_words[0].rearrange("p n i -> p (n i)").bitcast(I32))
+
+        planes = [sb("planes%d" % a, [P, S + H], U8) for a in range(2)]
+        w3_s = sb("w3_s", [P, N], U8)
+        for plane in planes + [w3_s]:
+            nc.gpsimd.memset(plane[:].bitcast(I32), 0)
+
+        stage = sb("stage", [P, S + H], U8)
+        nc.vector.tensor_copy(stage[:, W2_COL:W3_COL].rearrange("p (t m) -> p t m", t=4),
+                              w2s_raw[:].rearrange("p (m t) -> p t m", t=4))
+        v_scales = sb("v_scales", [P, S], U8)
+        nc.vector.tensor_copy(v_scales[:], scale_win[:].indirect(idx[:]))
+        nc.vector.tensor_copy(stage[:, 0:S].bitcast(I32), v_scales[:].bitcast(I32))
+        for a in range(2):
+            for q in range(4):
+                row = 16 * a + 4 * q
+                nc.gpsimd.dma_start(planes[a][32 * q:32 * q + 4, :].bitcast(I32),
+                                    stage[row:row + 4, :].bitcast(I32))
+        w3s_dealt = sb("w3s_dealt", [P, N], U8)
+        nc.vector.tensor_copy(w3s_dealt[:].rearrange("p (g t m) -> p g t m", g=2, t=4),
+                              w3s_raw[:].rearrange("p (g m t) -> p g t m", g=2, t=4))
+        for q in range(4):
+            nc.gpsimd.dma_start(w3_s[32 * q:32 * q + 4, :].bitcast(I32), w3s_dealt[4 * q:4 * q + 4, :].bitcast(I32))
+
+        v = [sb("v%d" % a, [P, S], U32) for a in range(2)]
+
+        def gather_v(a, half):
+            nc.vector.tensor_copy(v[a][:, BANK * half:BANK * (half + 1)],
+                                  tab[a][:].bitcast(U32).indirect(idx[:, 32 * half:32 * (half + 1)]))
+
+        def mm(acc, lhs, lhs_scale, rhs, rhs_scale, start, stop):
+            nc.tensor.matmul_mx(out=acc, lhsT=lhs, lhsT_scale=lhs_scale, rhs=rhs, rhs_scale=rhs_scale,
+                                start=start, stop=stop)
+
+        def v_pass(acc, lhs, lhs_scale, a, half, start, stop):
+            cols = slice(BANK * half, BANK * (half + 1))
+            mm(acc, lhs, lhs_scale, v[a][:, cols].bitcast(FP8X4), planes[a][:, cols], start, stop)
+
+        gather_v(0, 0)
+        gather_v(0, 1)
+        w2 = sb("w2", [P, 2, 2 * H], U8)
+        nc.vector.tensor_copy(w2[:].rearrange("p a (t m b) -> p a t m b", t=4, b=2),
+                              w2_raw[:].rearrange("p a (m t b) -> p a t m b", t=4, b=2))
+        gather_v(1, 0)
+        gather_v(1, 1)
+
+        w4_load(1, 0, "big0")
+        w4_load(1, 1, "big1")
+
+        units = [(half, t) for half in range(2) for t in range(4)]
+        acc = [bank(u, "trend%d" % u) for u in range(8)]
+        tg = [sb("tg%d" % half, [P, 4, BANK], F32) for half in range(2)]
+        passes = [(4 * half + t, half, t, a) for half in range(2) for a in range(2) for t in range(4)]
+        for u, half, t, a in passes:
+            if True:
+                v_pass(acc[u][:], w2[:, a, 256 * t:256 * (t + 1)].bitcast(FP4X4),
+                       planes[a][:, W2_COL + P * t:W2_COL + P * (t + 1)], a, half, a == 0, a == 1)
+        for u, (half, t) in enumerate(units):
+            nc.scalar.activation(tg[half][:, t, :], acc[u][:], ACT.Copy, scale=gains[:, t:t + 1])
+
+        def deal(copy, dst, raw, t0, nt, m0, nm):
+            copy(dst.rearrange("p (t m j) -> p m j t", t=nt, j=4)[:, m0:m0 + nm],
+                 raw.rearrange("p j (m t) -> p m j t", t=4)[:, m0:m0 + nm, :, t0:t0 + nt])
+
+        def quantise(codes, scales, values):
+            nc.vector.quantize_mx(out=codes.bitcast(FP8X4), scales=scales, in_=values)
+
+        w1_bf = [sb("w1_bf%d" % a, [P, 4 * H], BF16) for a in range(2)]
+        w1_q = [sb("w1_q%d" % a, [P, H], U32) for a in range(2)]
+        w1_s = [sb("w1_s%d" % a, [P, H], U8) for a in range(2)]
+        deal(nc.vector.tensor_copy, w1_bf[0][:], w1_raw[0][:], 0, 4, 0, P)
+        deal(nc.vector.tensor_copy, w1_bf[1][:], w1_raw[1][:], 0, 4, 0, 64)
+        quantise(w1_q[0][:], w1_s[0][:], w1_bf[0][:])
+        deal(nc.vector.tensor_copy, w1_bf[1][:], w1_raw[1][:], 0, 4, 64, 64)
+        for t in range(4):
+            quantise(w1_q[1][:, P * t:P * (t + 1)], w1_s[1][:, P * t:P * (t + 1)], w1_bf[1][:, BANK * t:BANK * (t + 1)])
+
+        y = []
+        for g in range(2):
+            y.append(sb("y%d" % g, [P, 4, M], F32, tag="mid%d" % g))
+            nc.sync.dma_start(y[g][:], base.rearrange("(g p t) m -> g p t m", g=2, t=4)[g])
+
+        acc = [bank(u, "width%d" % u) for u in range(8)]
+        for u, half, t, a in passes:
+            if True:
+                v_pass(acc[u][:], w1_q[a][:, P * t:P * (t + 1)].bitcast(FP8X4), w1_s[a][:, P * t:P * (t + 1)],
+                       a, half, a == 0, a == 1)
+        root = [sb("root%d" % half, [P, 4, BANK], F32) for half in range(2)]
+        for half in range(2):
+            for t in range(4):
+                nc.scalar.activation(root[half][:, t, :], acc[4 * half + t][:], ACT.Abs)
+            for c0, cw in H_CHUNKS:
+                if c0 // BANK == half:
+                    part = root[half][:, :, c0 % BANK:c0 % BANK + cw]
+                    nc.scalar.activation(part, part, ACT.Sqrt)
+
+        w3 = sb("w3", [P, N], I32)
+        nc.vector.tensor_copy(w3[:].rearrange("p (g t m) -> p g m t", g=2, t=4),
+                              w3_raw[:].rearrange("p (g m t) -> p g m t", g=2, t=4))
+        w4_q = [[sb("w4_q%d%d" % (g, a), [P, BANK], U32) for a in range(2)] for g in range(2)]
+        w4_s = [[sb("w4_s%d%d" % (g, a), [P, BANK], U8) for a in range(2)] for g in range(2)]
+        w4_bf = {}
+
+        def w4_round(copy, g, a, t0, nt, tag=None):
+            w4_bf[g, a, t0] = sb("w4_bf%d%d%d" % (g, a, t0), [P, BANK * nt], BF16, tag=tag)
+            deal(copy, w4_bf[g, a, t0][:], w4_raw[g, a][:], t0, nt, 0, P)
+
+        def w4_quantise(g, a, t0, nt):
+            cols = slice(P * t0, P * (t0 + nt))
+            quantise(w4_q[g][a][:, cols], w4_s[g][a][:, cols], w4_bf[g, a, t0][:])
+
+        h_bf = sb("h_bf", [P, 4 * S], BF16)
+        h_q = sb("h_q", [P, S], U32)
+        h_s = sb("h_s", [P, S], U8)
+
+        def h_make(c0, cw):
+            nc.vector.tensor_tensor(h_bf[:, 4 * c0:4 * (c0 + cw)].rearrange("p (c i t) -> p c t i", i=4, t=4),
+                                    root[c0 // BANK][:, :, c0 % BANK:c0 % BANK + cw].rearrange("p t (c i) -> p c t i", i=4),
+                                    tg[c0 // BANK][:, :, c0 % BANK:c0 % BANK + cw].rearrange("p t (c i) -> p c t i", i=4), MULT)
+
+        def h_quantise(c0, cw):
+            quantise(h_q[:, c0:c0 + cw], h_s[:, c0:c0 + cw], h_bf[:, 4 * c0:4 * (c0 + cw)])
+
+        w4_round(nc.vector.tensor_copy, 0, 0, 0, 2)
+        h_make(*H_CHUNKS[0])
+        w4_quantise(0, 0, 0, 2)
+        w4_round(nc.vector.tensor_copy, 0, 1, 0, 2)
+        h_quantise(*H_CHUNKS[0])
+        h_make(*H_CHUNKS[1])
+        w4_quantise(0, 1, 0, 2)
+        for c in range(1, len(H_CHUNKS)):
+            h_quantise(*H_CHUNKS[c])
+            if c + 1 < len(H_CHUNKS):
+                h_make(*H_CHUNKS[c + 1])
+
+        feat = {}
+
+        def features(s):
+            g, t = divmod(s, 4)
+            feat[s] = sb("feat%d" % s, [P, S], F32)
+            cols = slice(P * t, P * (t + 1))
+            n0 = BANK * g + P * t
+            for half in range(2):
+                out = bank((2 * s + half) % 8, "f%d%d" % (s, half))
+                for a in range(2):
+                    v_pass(out[:], w4_q[g][a][:, cols].bitcast(FP8X4), w4_s[g][a][:, cols], a, half, a == 0, False)
+                pieces = [c for c in H_CHUNKS if c[0] // BANK == half] if s == 0 else [(BANK * half, BANK)]
+                for c0, cw in pieces:
+                    mm(out[:, c0 - BANK * half:c0 - BANK * half + cw], w3[:, n0:n0 + P].bitcast(FP8X4),
+                       w3_s[:, n0:n0 + P], h_q[:, c0:c0 + cw].bitcast(FP8X4),
+                       h_s[:, c0:c0 + cw], False, (c0, cw) == pieces[-1])
+                nc.scalar.copy(feat[s][:, BANK * half:BANK * (half + 1)], out[:])
+
+        y_rows = out_0.rearrange("(g p t) m -> g p t m", g=2, t=4)
+        y_bf = [sb("y_bf%d" % g, [P, 4 * M], BF16) for g in range(2)]
+        y_q = [sb("y_q%d" % g, [P, M], I32) for g in range(2)]
+        y_s = sb("y_s", [P, 2, M], U8)
+        first, prod = {}, {}
+
+        def pick(job):
+            s, m0, mw = job
+            first[job] = ring.tile([P, mw], F32, name="first", tag="first")
+            nc.vector.tensor_copy(first[job][:], feat[s][:].indirect(p1[:, m0 // 16:(m0 + mw) // 16]))
+
+        def multiply(job):
+            s, m0, mw = job
+            prod[job] = ring.tile([P, mw], F32, name="prod", tag="prod")
+            nc.vector.tensor_tensor(prod[job][:], feat[s][:].indirect(p2[:, m0 // 16:(m0 + mw) // 16]), first[job][:], MULT)
+
+        def add_base(job):
+            s, m0, mw = job
+            g, t = divmod(s, 4)
+            nc.vector.tensor_tensor(y[g][:, t, m0:m0 + mw], prod[job][:], y[g][:, t, m0:m0 + mw], ADD)
+            nc.sync.dma_start(y_rows[g][:, t, m0:m0 + mw], y[g][:, t, m0:m0 + mw])
+
+        def y_round(copy, g, m0, mw):
+            copy(y_bf[g][:, 4 * m0:4 * (m0 + mw)].rearrange("p (c i t) -> p c t i", i=4, t=4),
+                 y[g][:, :, m0:m0 + mw].rearrange("p t (c i) -> p c t i", i=4))
+
+        def y_quantise(g, m0, mw):
+            quantise(y_q[g][:, m0:m0 + mw], y_s[:, g, m0:m0 + mw], y_bf[g][:, 4 * m0:4 * (m0 + mw)])
+            nc.sync.dma_start(out_1[g].rearrange("p m t -> p (m t)").bitcast(I32)[:, m0:m0 + mw], y_q[g][:, m0:m0 + mw])
+
+        jobs = [(s, 0, M) for s in range(7)] + [(7, 0, 256), (7, 256, 256)]
+        features(0)
+        features(1)
+        for a in range(2):
+            w4_round(nc.scalar.copy, 0, a, 2, 2, ("tg0", "root0")[a])
+        pick(jobs[0])
+        for i, job in enumerate(jobs):
+            if i == 0:
+                for a in range(2):
+                    w4_quantise(0, a, 2, 2)
+                features(2)
+                features(3)
+                for a in range(2):
+                    w4_round(nc.scalar.copy, 1, a, 0, 4, ("tg1", "root1")[a])
+            if i == 2:
+                for a in range(2):
+                    w4_quantise(1, a, 0, 4)
+                for s in range(4, 8):
+                    features(s)
+            if i + 1 < len(jobs):
+                pick(jobs[i + 1])
+            if i > 0:
+                add_base(jobs[i - 1])
+            multiply(job)
+            if i == 4:
+                y_round(nc.scalar.copy, 0, 0, M)
+            if i == 6:
+                y_quantise(0, 0, M)
+        y_round(nc.scalar.copy, 1, 0, 256)
+        add_base(jobs[-1])
+        y_round(nc.scalar.copy, 1, 256, 64)
+        y_round(nc.vector.tensor_copy, 1, 320, 192)
+        y_quantise(1, 0, 256)
+        y_quantise(1, 256, 256)
+        for q in range(4):
+            queue = nc.scalar if q % 2 else nc.sync
+            queue.dma_start(out_2[:, 4 * q:4 * q + 4, :].rearrange("g r m -> r g m").bitcast(I32),
+                            y_s[32 * q:32 * q + 4].bitcast(I32))

@@ -20,6 +20,7 @@ ADD = mybir.AluOpType.add
 P = 128
 BANK = 512
 H_CHUNKS = [(0, 256), (256, 256), (512, 256), (768, 128), (896, 128)]
+SHARED = (0, 1, 2, 3, 4, 5, 6)
 W2_COL = S
 W3_COL = S + H
 
@@ -30,11 +31,15 @@ def tile_list_ring_window_pairs_kernel(tc, tab_words, tab_scales, offs, w1, w2_w
     with ExitStack() as ctx:
         lists = ctx.enter_context(tc.tile_pool(name="lists", bufs=1))
         keep = ctx.enter_context(tc.tile_pool(name="keep", bufs=1))
-        ring = ctx.enter_context(tc.tile_pool(name="ring", bufs=3))
+        ring = ctx.enter_context(tc.tile_pool(name="ring", bufs=4))
+        placed = ctx.enter_context(tc.tile_pool(name="placed", bufs=1))
         psum = ctx.enter_context(tc.psum_pool(name="psum", bufs=1))
 
         def sb(name, shape, dtype, tag=None):
             return keep.tile(shape, dtype, name=name, tag=tag or name, align_bytes=64)
+
+        def at(offset, name, shape, dtype):
+            return placed.tile(shape, dtype, name=name, align_bytes=64, offset=offset)
 
         def bank(i, name):
             return psum.tile([P, BANK], F32, name=name, tag="bank%d" % i)
@@ -45,66 +50,56 @@ def tile_list_ring_window_pairs_kernel(tc, tab_words, tab_scales, offs, w1, w2_w
         nc.scalar.dma_start(scale_win[0:32, :].bitcast(I32), tab_scales.rearrange("a q t -> (a q) t").bitcast(I32))
         w2s_raw = sb("w2s_raw", [P, H], U8)
         nc.scalar.dma_start(w2s_raw[0:32, :].bitcast(I32), w2_scales.rearrange("a q c -> (a q) c").bitcast(I32))
-        nc.vector.memset(w2s_raw[32:64, :].bitcast(I32), 0)
-        nc.vector.memset(w2s_raw[64:128, :].bitcast(I32), 0)
-        w3s_raw = sb("w3s_raw", [P, N], U8)
-        nc.vector.memset(w3s_raw[:].bitcast(I32), 0)
         warm = sb("warm", [P, 2], F32)
         nc.vector.memset(warm[:], 1.0)
-        nc.vector.memset(scale_win[32:64, :].bitcast(I32), 0)
-        nc.vector.memset(scale_win[64:128, :].bitcast(I32), 0)
-        tab = []
-        for a in range(2):
-            tab.append(sb("tab%d" % a, [P, T], I32, tag="big%d" % a))
-            nc.sync.dma_start(tab[a][:], tab_words[a].rearrange("p n i -> p (n i)").bitcast(I32))
-        w2_raw = sb("w2_raw", [P, 2, 2 * H], U8)
-        nc.scalar.dma_start(w2_raw[:].bitcast(I32), w2_words.rearrange("a p c -> p a c").bitcast(I32))
-        gains = sb("gains", [P, 4], F32)
-        nc.scalar.dma_start(gains[:], gain.rearrange("(p t) -> p t", t=4))
-        nc.scalar.dma_start(w3s_raw[0:16, :].bitcast(I32), w3_scales[0].bitcast(I32))
-        nc.scalar.activation(warm[:, 1:2], warm[:, 0:1], ACT.Sqrt)
-        w1_raw = [sb("w1_raw%d" % a, [P, 4, H], F32, tag="mid%d" % a) for a in range(2)]
-        w1_rows = w1.rearrange("(a p j) c -> a p j c", a=2, j=4)
-        nc.sync.dma_start(w1_raw[0][:], w1_rows[0])
-        for c in range(2):
-            nc.sync.dma_start(w1_raw[1][:, :, 256 * c:256 * (c + 1)], w1_rows[1][:, :, 256 * c:256 * (c + 1)])
+        for rows in (slice(32, 64), slice(64, 128)):
+            nc.vector.memset(w2s_raw[rows, :].bitcast(I32), 0)
+            nc.vector.memset(scale_win[rows, :].bitcast(I32), 0)
         p1 = lists.tile([P, M // 16], U16, name="p1")
         nc.sync.dma_start(p1[:], pos1)
         p2 = lists.tile([P, M // 16], U16, name="p2")
         nc.sync.dma_start(p2[:], pos2)
-        w4_rows = w4.rearrange("(a p j) c -> a p j c", a=2, j=4)
-        w4_raw = {}
-
-        def w4_load(g, a, tag):
-            w4_raw[g, a] = sb("w4_raw%d%d" % (g, a), [P, 4, BANK], F32, tag=tag)
-            nc.sync.dma_start(w4_raw[g, a][:], w4_rows[a][:, :, BANK * g:BANK * (g + 1)])
-
-        w4_load(0, 0, None)
-        w4_load(0, 1, None)
-        w3_raw = sb("w3_raw", [P, N], I32)
-        nc.sync.dma_start(w3_raw[:], w3_words[0].rearrange("p n i -> p (n i)").bitcast(I32))
+        w2_raw = sb("w2_raw", [P, 2, 2 * H], U8)
+        nc.scalar.dma_start(w2_raw[:].bitcast(I32), w2_words.rearrange("a p c -> p a c").bitcast(I32))
+        gains = sb("gains", [P, 4], F32)
+        nc.scalar.dma_start(gains[:], gain.rearrange("(p t) -> p t", t=4))
+        tab = [sb("tab0", [P, T], I32, tag="big0")]
+        nc.sync.dma_start(tab[0][:], tab_words[0].rearrange("p n i -> p (n i)").bitcast(I32))
+        w1_rows = w1.rearrange("(a p j) c -> a p j c", a=2, j=4)
+        w1_raw = [sb("w1_raw0", [P, 4, H], F32, tag="mid")[:]]
+        nc.sync.dma_start(w1_raw[0], w1_rows[0])
+        nc.scalar.activation(warm[:, 1:2], warm[:, 0:1], ACT.Sqrt)
 
         planes = [sb("planes%d" % a, [P, S + H], U8) for a in range(2)]
-        w3_s = sb("w3_s", [P, N], U8)
-        for plane in planes + [w3_s]:
-            nc.gpsimd.memset(plane[:].bitcast(I32), 0)
-
-        stage = sb("stage", [P, S + H], U8)
-        nc.vector.tensor_copy(stage[:, W2_COL:W3_COL].rearrange("p (t m) -> p t m", t=4),
+        nc.vector.tensor_copy(planes[0][:, W2_COL:W3_COL].rearrange("p (t m) -> p t m", t=4),
                               w2s_raw[:].rearrange("p (m t) -> p t m", t=4))
-        v_scales = sb("v_scales", [P, S], U8)
+        nc.vector.tensor_copy(planes[1][:, W2_COL:W3_COL].bitcast(I32), planes[0][:, W2_COL:W3_COL].bitcast(I32))
+        v_scales = at(4 * T - S // 2, "v_scales", [P, S], U8)
         nc.vector.tensor_copy(v_scales[:], scale_win[:].indirect(idx[:]))
-        nc.vector.tensor_copy(stage[:, 0:S].bitcast(I32), v_scales[:].bitcast(I32))
+        for a in range(2):
+            nc.vector.tensor_copy(planes[a][:, 0:S].bitcast(I32), v_scales[:].bitcast(I32))
         for a in range(2):
             for q in range(4):
                 row = 16 * a + 4 * q
-                nc.gpsimd.dma_start(planes[a][32 * q:32 * q + 4, :].bitcast(I32),
-                                    stage[row:row + 4, :].bitcast(I32))
-        w3s_dealt = sb("w3s_dealt", [P, N], U8)
-        nc.vector.tensor_copy(w3s_dealt[:].rearrange("p (g t m) -> p g t m", g=2, t=4),
-                              w3s_raw[:].rearrange("p (g m t) -> p g t m", g=2, t=4))
+                if row != 32 * q:
+                    queue = nc.gpsimd if row == 28 else nc.sync
+                    queue.dma_start(planes[a][32 * q:32 * q + 4, :].bitcast(I32), planes[a][row:row + 4, :].bitcast(I32))
+        tab.append(at(0, "tab1", [P, T], I32))
+        nc.sync.dma_start(tab[1][:], tab_words[1].rearrange("p n i -> p (n i)").bitcast(I32))
+        w1_raw.append(at(4 * T, "w1_raw1", [P, 4, H], F32)[:])
+        for c in range(2):
+            nc.sync.dma_start(w1_raw[1][:, :, 256 * c:256 * (c + 1)], w1_rows[1][:, :, 256 * c:256 * (c + 1)])
+        w3s_raw = sb("w3s_raw", [P, N], U8)
+        nc.gpsimd.memset(w3s_raw[:].bitcast(I32), 0)
         for q in range(4):
-            nc.gpsimd.dma_start(w3_s[32 * q:32 * q + 4, :].bitcast(I32), w3s_dealt[4 * q:4 * q + 4, :].bitcast(I32))
+            nc.gpsimd.dma_start(w3s_raw[32 * q:32 * q + 4, :].bitcast(I32), w3_scales[0][4 * q:4 * q + 4, :].bitcast(I32))
+
+        w4_rows = w4.rearrange("(a p j) c -> a p j c", a=2, j=4)
+        w4_raw = {}
+
+        def w4_load(g, a, tile):
+            w4_raw[g, a] = tile
+            nc.sync.dma_start(tile, w4_rows[a][:, :, BANK * g:BANK * (g + 1)])
 
         v = [sb("v%d" % a, [P, S], U32) for a in range(2)]
 
@@ -128,19 +123,12 @@ def tile_list_ring_window_pairs_kernel(tc, tab_words, tab_scales, offs, w1, w2_w
         gather_v(1, 0)
         gather_v(1, 1)
 
-        w4_load(1, 0, "big0")
-        w4_load(1, 1, "big1")
-
-        units = [(half, t) for half in range(2) for t in range(4)]
-        acc = [bank(u, "trend%d" % u) for u in range(8)]
-        tg = [sb("tg%d" % half, [P, 4, BANK], F32) for half in range(2)]
-        passes = [(4 * half + t, half, t, a) for half in range(2) for a in range(2) for t in range(4)]
-        for u, half, t, a in passes:
-            if True:
-                v_pass(acc[u][:], w2[:, a, 256 * t:256 * (t + 1)].bitcast(FP4X4),
-                       planes[a][:, W2_COL + P * t:W2_COL + P * (t + 1)], a, half, a == 0, a == 1)
-        for u, (half, t) in enumerate(units):
-            nc.scalar.activation(tg[half][:, t, :], acc[u][:], ACT.Copy, scale=gains[:, t:t + 1])
+        w4_first = sb("w4_first", [P, 2, 4, BANK], F32, tag="big0")
+        for a in range(2):
+            w4_load(0, a, w4_first[:, a])
+        w3_s = sb("w3_s", [P, N], U8)
+        nc.vector.tensor_copy(w3_s[:].rearrange("p (g t m) -> p g t m", g=2, t=4),
+                              w3s_raw[:].rearrange("p (g m t) -> p g t m", g=2, t=4))
 
         def deal(copy, dst, raw, t0, nt, m0, nm):
             copy(dst.rearrange("p (t m j) -> p m j t", t=nt, j=4)[:, m0:m0 + nm],
@@ -152,17 +140,36 @@ def tile_list_ring_window_pairs_kernel(tc, tab_words, tab_scales, offs, w1, w2_w
         w1_bf = [sb("w1_bf%d" % a, [P, 4 * H], BF16) for a in range(2)]
         w1_q = [sb("w1_q%d" % a, [P, H], U32) for a in range(2)]
         w1_s = [sb("w1_s%d" % a, [P, H], U8) for a in range(2)]
-        deal(nc.vector.tensor_copy, w1_bf[0][:], w1_raw[0][:], 0, 4, 0, P)
-        deal(nc.vector.tensor_copy, w1_bf[1][:], w1_raw[1][:], 0, 4, 0, 64)
+        deal(nc.scalar.copy, w1_bf[0][:], w1_raw[0], 0, 4, 0, P)
         quantise(w1_q[0][:], w1_s[0][:], w1_bf[0][:])
-        deal(nc.vector.tensor_copy, w1_bf[1][:], w1_raw[1][:], 0, 4, 64, 64)
+        w3_raw = sb("w3_raw", [P, N], I32, tag="mid")
+        nc.sync.dma_start(w3_raw[:], w3_words[0].rearrange("p n i -> p (n i)").bitcast(I32))
+
+        units = [(half, t) for half in range(2) for t in range(4)]
+        acc = [bank(u, "trend%d" % u) for u in range(8)]
+        tg = [sb("tg%d" % half, [P, 4, BANK], F32) for half in range(2)]
+        passes = [(4 * half + t, half, t, a) for half in range(2) for a in range(2) for t in range(4)]
+        for u, half, t, a in passes:
+            if True:
+                v_pass(acc[u][:], w2[:, a, 256 * t:256 * (t + 1)].bitcast(FP4X4),
+                       planes[a][:, W2_COL + P * t:W2_COL + P * (t + 1)], a, half, a == 0, a == 1)
+        for u, (half, t) in enumerate(units[:6]):
+            nc.scalar.activation(tg[half][:, t, :], acc[u][:], ACT.Copy, scale=gains[:, t:t + 1])
+
+        deal(nc.vector.tensor_copy, w1_bf[1][:], w1_raw[1], 0, 4, 0, 64)
+        deal(nc.vector.tensor_copy, w1_bf[1][:], w1_raw[1], 0, 4, 64, 64)
         for t in range(4):
             quantise(w1_q[1][:, P * t:P * (t + 1)], w1_s[1][:, P * t:P * (t + 1)], w1_bf[1][:, BANK * t:BANK * (t + 1)])
 
-        y = []
+        for u in (6, 7):
+            half, t = units[u]
+            nc.vector.tensor_scalar(tg[half][:, t, :], acc[u][:], gains[:, t:t + 1], None, MULT)
+        for a in range(2):
+            w4_load(1, a, sb("w4_raw1%d" % a, [P, 4, BANK], F32, tag="w1_bf%d" % a)[:])
+        y = [at(4 * T * g, "y%d" % g, [P, 4, M], F32)[:] for g in range(2)]
+        base_rows = base.rearrange("(g p t) m -> g p t m", g=2, t=4)
         for g in range(2):
-            y.append(sb("y%d" % g, [P, 4, M], F32, tag="mid%d" % g))
-            nc.sync.dma_start(y[g][:], base.rearrange("(g p t) m -> g p t m", g=2, t=4)[g])
+            nc.sync.dma_start(y[g], base_rows[g])
 
         acc = [bank(u, "width%d" % u) for u in range(8)]
         for u, half, t, a in passes:
@@ -170,11 +177,13 @@ def tile_list_ring_window_pairs_kernel(tc, tab_words, tab_scales, offs, w1, w2_w
                 v_pass(acc[u][:], w1_q[a][:, P * t:P * (t + 1)].bitcast(FP8X4), w1_s[a][:, P * t:P * (t + 1)],
                        a, half, a == 0, a == 1)
         root = [sb("root%d" % half, [P, 4, BANK], F32) for half in range(2)]
-        for half in range(2):
+        for a0, aw in [(0, 512), (512, 256), (768, 256)]:
+            half = a0 // BANK
+            cols = slice(a0 % BANK, a0 % BANK + aw)
             for t in range(4):
-                nc.scalar.activation(root[half][:, t, :], acc[4 * half + t][:], ACT.Abs)
+                nc.scalar.activation(root[half][:, t, cols], acc[4 * half + t][:, cols], ACT.Abs)
             for c0, cw in H_CHUNKS:
-                if c0 // BANK == half:
+                if a0 <= c0 < a0 + aw:
                     part = root[half][:, :, c0 % BANK:c0 % BANK + cw]
                     nc.scalar.activation(part, part, ACT.Sqrt)
 
@@ -186,12 +195,16 @@ def tile_list_ring_window_pairs_kernel(tc, tab_words, tab_scales, offs, w1, w2_w
         w4_bf = {}
 
         def w4_round(copy, g, a, t0, nt, tag=None):
-            w4_bf[g, a, t0] = sb("w4_bf%d%d%d" % (g, a, t0), [P, BANK * nt], BF16, tag=tag)
-            deal(copy, w4_bf[g, a, t0][:], w4_raw[g, a][:], t0, nt, 0, P)
+            if (g, t0) == (1, 2):
+                w4_bf[g, a, t0] = w4_bf[g, a, "whole"][:, 2 * BANK:]
+            else:
+                w4_bf[g, a, "whole"] = sb("w4_bf%d%d%d" % (g, a, t0), [P, 4 * BANK if g else 2 * BANK], BF16, tag=tag)
+                w4_bf[g, a, t0] = w4_bf[g, a, "whole"][:, 0:2 * BANK]
+            deal(copy, w4_bf[g, a, t0], w4_raw[g, a], t0, nt, 0, P)
 
         def w4_quantise(g, a, t0, nt):
             cols = slice(P * t0, P * (t0 + nt))
-            quantise(w4_q[g][a][:, cols], w4_s[g][a][:, cols], w4_bf[g, a, t0][:])
+            quantise(w4_q[g][a][:, cols], w4_s[g][a][:, cols], w4_bf[g, a, t0])
 
         h_bf = sb("h_bf", [P, 4 * S], BF16)
         h_q = sb("h_q", [P, S], U32)
@@ -233,28 +246,36 @@ def tile_list_ring_window_pairs_kernel(tc, tab_words, tab_scales, offs, w1, w2_w
                     mm(out[:, c0 - BANK * half:c0 - BANK * half + cw], w3[:, n0:n0 + P].bitcast(FP8X4),
                        w3_s[:, n0:n0 + P], h_q[:, c0:c0 + cw].bitcast(FP8X4),
                        h_s[:, c0:c0 + cw], False, (c0, cw) == pieces[-1])
-                nc.scalar.copy(feat[s][:, BANK * half:BANK * (half + 1)], out[:])
+                copy = nc.vector.tensor_copy if (s, half) == (0, 1) else nc.scalar.copy
+                copy(feat[s][:, BANK * half:BANK * (half + 1)], out[:])
 
         y_rows = out_0.rearrange("(g p t) m -> g p t m", g=2, t=4)
         y_bf = [sb("y_bf%d" % g, [P, 4 * M], BF16) for g in range(2)]
         y_q = [sb("y_q%d" % g, [P, M], I32) for g in range(2)]
         y_s = sb("y_s", [P, 2, M], U8)
-        first, prod = {}, {}
+        first, second, prod = {}, {}, {}
 
         def pick(job):
             s, m0, mw = job
             first[job] = ring.tile([P, mw], F32, name="first", tag="first")
             nc.vector.tensor_copy(first[job][:], feat[s][:].indirect(p1[:, m0 // 16:(m0 + mw) // 16]))
+            if s in SHARED:
+                second[job] = ring.tile([P, mw], F32, name="second", tag="second")
+                nc.vector.tensor_copy(second[job][:], feat[s][:].indirect(p2[:, m0 // 16:(m0 + mw) // 16]))
 
         def multiply(job):
             s, m0, mw = job
             prod[job] = ring.tile([P, mw], F32, name="prod", tag="prod")
+            if s in SHARED:
+                nc.gpsimd.tensor_tensor(prod[job][:], second[job][:], first[job][:], MULT)
+                return
             nc.vector.tensor_tensor(prod[job][:], feat[s][:].indirect(p2[:, m0 // 16:(m0 + mw) // 16]), first[job][:], MULT)
 
         def add_base(job):
             s, m0, mw = job
             g, t = divmod(s, 4)
-            nc.vector.tensor_tensor(y[g][:, t, m0:m0 + mw], prod[job][:], y[g][:, t, m0:m0 + mw], ADD)
+            engine = nc.gpsimd if s in SHARED else nc.vector
+            engine.tensor_tensor(y[g][:, t, m0:m0 + mw], prod[job][:], y[g][:, t, m0:m0 + mw], ADD)
             nc.sync.dma_start(y_rows[g][:, t, m0:m0 + mw], y[g][:, t, m0:m0 + mw])
 
         def y_round(copy, g, m0, mw):
@@ -276,14 +297,21 @@ def tile_list_ring_window_pairs_kernel(tc, tab_words, tab_scales, offs, w1, w2_w
                 for a in range(2):
                     w4_quantise(0, a, 2, 2)
                 features(2)
+                for a in range(2):
+                    w4_round(nc.scalar.copy, 1, a, 0, 2, ("tg1", "root1")[a])
                 features(3)
+            if i == 1:
                 for a in range(2):
-                    w4_round(nc.scalar.copy, 1, a, 0, 4, ("tg1", "root1")[a])
-            if i == 2:
+                    w4_quantise(1, a, 0, 2)
+                features(4)
                 for a in range(2):
-                    w4_quantise(1, a, 0, 4)
-                for s in range(4, 8):
-                    features(s)
+                    w4_round(nc.scalar.copy, 1, a, 2, 2)
+                features(5)
+            if i == 3:
+                for a in range(2):
+                    w4_quantise(1, a, 2, 2)
+                features(6)
+                features(7)
             if i + 1 < len(jobs):
                 pick(jobs[i + 1])
             if i > 0:

@@ -20,7 +20,7 @@ ADD = mybir.AluOpType.add
 P = 128
 BANK = 512
 H_CHUNKS = [(0, 256), (256, 256), (512, 256), (768, 128), (896, 128)]
-SHARED = (0, 1, 2, 3, 4, 5, 6)
+SHARED = ()
 W2_COL = S
 W3_COL = S + H
 
@@ -153,7 +153,7 @@ def tile_list_ring_window_pairs_kernel(tc, tab_words, tab_scales, offs, w1, w2_w
             if True:
                 v_pass(acc[u][:], w2[:, a, 256 * t:256 * (t + 1)].bitcast(FP4X4),
                        planes[a][:, W2_COL + P * t:W2_COL + P * (t + 1)], a, half, a == 0, a == 1)
-        for u, (half, t) in enumerate(units[:6]):
+        for u, (half, t) in enumerate(units[:7]):
             nc.scalar.activation(tg[half][:, t, :], acc[u][:], ACT.Copy, scale=gains[:, t:t + 1])
 
         deal(nc.vector.tensor_copy, w1_bf[1][:], w1_raw[1], 0, 4, 0, 64)
@@ -161,7 +161,7 @@ def tile_list_ring_window_pairs_kernel(tc, tab_words, tab_scales, offs, w1, w2_w
         for t in range(4):
             quantise(w1_q[1][:, P * t:P * (t + 1)], w1_s[1][:, P * t:P * (t + 1)], w1_bf[1][:, BANK * t:BANK * (t + 1)])
 
-        for u in (6, 7):
+        for u in (7,):
             half, t = units[u]
             nc.vector.tensor_scalar(tg[half][:, t, :], acc[u][:], gains[:, t:t + 1], None, MULT)
         for a in range(2):
@@ -286,7 +286,7 @@ def tile_list_ring_window_pairs_kernel(tc, tab_words, tab_scales, offs, w1, w2_w
             quantise(y_q[g][:, m0:m0 + mw], y_s[:, g, m0:m0 + mw], y_bf[g][:, 4 * m0:4 * (m0 + mw)])
             nc.sync.dma_start(out_1[g].rearrange("p m t -> p (m t)").bitcast(I32)[:, m0:m0 + mw], y_q[g][:, m0:m0 + mw])
 
-        jobs = [(s, 0, M) for s in range(7)] + [(7, 0, 256), (7, 256, 256)]
+        jobs = [(s, 0, M) for s in range(7)] + [(7, 0, 256), (7, 256, 128), (7, 384, 128)]
         features(0)
         features(1)
         for a in range(2):
@@ -321,11 +321,12 @@ def tile_list_ring_window_pairs_kernel(tc, tab_words, tab_scales, offs, w1, w2_w
                 y_round(nc.scalar.copy, 0, 0, M)
             if i == 6:
                 y_quantise(0, 0, M)
-        y_round(nc.scalar.copy, 1, 0, 256)
+            if i == 8:
+                y_round(nc.scalar.copy, 1, 0, 256)
+        y_round(nc.scalar.copy, 1, 256, 128)
         add_base(jobs[-1])
-        y_round(nc.scalar.copy, 1, 256, 64)
-        y_round(nc.vector.tensor_copy, 1, 320, 192)
         y_quantise(1, 0, 256)
+        y_round(nc.vector.tensor_copy, 1, 384, 128)
         y_quantise(1, 256, 256)
         for q in range(4):
             queue = nc.scalar if q % 2 else nc.sync

from contextlib import ExitStack

import concourse.mybir as mybir

K, T, S, H, N, M = 1024, 4096, 1024, 512, 1024, 512
FLOPS = 5368709120

F32 = mybir.dt.float32
BF16 = mybir.dt.bfloat16
I32 = mybir.dt.int32
U32 = mybir.dt.uint32
U16 = mybir.dt.uint16
U8 = mybir.dt.uint8
FP8X4 = mybir.dt.float8_e4m3fn_x4
FP4X4 = mybir.dt.float4_e2m1fn_x4
ACT = mybir.ActivationFunctionType
MULT = mybir.AluOpType.mult
ADD = mybir.AluOpType.add

P = 128
BANK = 512
H_CHUNKS = [(0, 256), (256, 256), (512, 256), (768, 128), (896, 128)]
SHARED = ()
W2_COL = S
W3_COL = S + H


def tile_list_ring_window_pairs_kernel(tc, tab_words, tab_scales, offs, w1, w2_words, w2_scales, gain,
                                                 w3_words, w3_scales, w4, pos1, pos2, base, out_0, out_1, out_2):
    nc = tc.nc
    with ExitStack() as ctx:
        lists = ctx.enter_context(tc.tile_pool(name="lists", bufs=1))
        keep = ctx.enter_context(tc.tile_pool(name="keep", bufs=1))
        ring = ctx.enter_context(tc.tile_pool(name="ring", bufs=4))
        placed = ctx.enter_context(tc.tile_pool(name="placed", bufs=1))
        psum = ctx.enter_context(tc.psum_pool(name="psum", bufs=1))

        def sb(name, shape, dtype, tag=None):
            return keep.tile(shape, dtype, name=name, tag=tag or name, align_bytes=64)

        def at(offset, name, shape, dtype):
            return placed.tile(shape, dtype, name=name, align_bytes=64, offset=offset)

        def bank(i, name):
            return psum.tile([P, BANK], F32, name=name, tag="bank%d" % i)

        idx = lists.tile([P, S // 16], U16, name="idx")
        nc.sync.dma_start(idx[:], offs)
        scale_win = sb("scale_win", [P, T], U8)
        nc.scalar.dma_start(scale_win[0:32, :].bitcast(I32), tab_scales.rearrange("a q t -> (a q) t").bitcast(I32))
        w2s_raw = sb("w2s_raw", [P, H], U8)
        nc.scalar.dma_start(w2s_raw[0:32, :].bitcast(I32), w2_scales.rearrange("a q c -> (a q) c").bitcast(I32))
        warm = sb("warm", [P, 2], F32)
        nc.vector.memset(warm[:], 1.0)
        for rows in (slice(32, 64), slice(64, 128)):
            nc.vector.memset(w2s_raw[rows, :].bitcast(I32), 0)
            nc.vector.memset(scale_win[rows, :].bitcast(I32), 0)
        p1 = lists.tile([P, M // 16], U16, name="p1")
        nc.sync.dma_start(p1[:], pos1)
        p2 = lists.tile([P, M // 16], U16, name="p2")
        nc.sync.dma_start(p2[:], pos2)
        w2_raw = sb("w2_raw", [P, 2, 2 * H], U8)
        nc.scalar.dma_start(w2_raw[:].bitcast(I32), w2_words.rearrange("a p c -> p a c").bitcast(I32))
        gains = sb("gains", [P, 4], F32)
        nc.scalar.dma_start(gains[:], gain.rearrange("(p t) -> p t", t=4))
        tab = [sb("tab0", [P, T], I32, tag="big0")]
        nc.sync.dma_start(tab[0][:], tab_words[0].rearrange("p n i -> p (n i)").bitcast(I32))
        w1_rows = w1.rearrange("(a p j) c -> a p j c", a=2, j=4)
        w1_raw = [sb("w1_raw0", [P, 4, H], F32, tag="mid")[:]]
        nc.sync.dma_start(w1_raw[0], w1_rows[0])
        nc.scalar.activation(warm[:, 1:2], warm[:, 0:1], ACT.Sqrt)

        planes = [sb("planes%d" % a, [P, S + H], U8) for a in range(2)]
        nc.vector.tensor_copy(planes[0][:, W2_COL:W3_COL].rearrange("p (t m) -> p t m", t=4),
                              w2s_raw[:].rearrange("p (m t) -> p t m", t=4))
        nc.vector.tensor_copy(planes[1][:, W2_COL:W3_COL].bitcast(I32), planes[0][:, W2_COL:W3_COL].bitcast(I32))
        v_scales = at(4 * T - S // 2, "v_scales", [P, S], U8)
        nc.vector.tensor_copy(v_scales[:], scale_win[:].indirect(idx[:]))
        for a in range(2):
            nc.vector.tensor_copy(planes[a][:, 0:S].bitcast(I32), v_scales[:].bitcast(I32))
        for a in range(2):
            for q in range(4):
                row = 16 * a + 4 * q
                if row != 32 * q:
                    queue = nc.gpsimd if row == 28 else nc.sync
                    queue.dma_start(planes[a][32 * q:32 * q + 4, :].bitcast(I32), planes[a][row:row + 4, :].bitcast(I32))
        tab.append(at(0, "tab1", [P, T], I32))
        nc.sync.dma_start(tab[1][:], tab_words[1].rearrange("p n i -> p (n i)").bitcast(I32))
        w1_raw.append(at(4 * T, "w1_raw1", [P, 4, H], F32)[:])
        for c in range(2):
            nc.sync.dma_start(w1_raw[1][:, :, 256 * c:256 * (c + 1)], w1_rows[1][:, :, 256 * c:256 * (c + 1)])
        w3s_raw = sb("w3s_raw", [P, N], U8)
        nc.gpsimd.memset(w3s_raw[:].bitcast(I32), 0)
        for q in range(4):
            nc.gpsimd.dma_start(w3s_raw[32 * q:32 * q + 4, :].bitcast(I32), w3_scales[0][4 * q:4 * q + 4, :].bitcast(I32))

        w4_rows = w4.rearrange("(a p j) c -> a p j c", a=2, j=4)
        w4_raw = {}

        def w4_load(g, a, tile):
            w4_raw[g, a] = tile
            nc.sync.dma_start(tile, w4_rows[a][:, :, BANK * g:BANK * (g + 1)])

        v = [sb("v%d" % a, [P, S], U32) for a in range(2)]

        def gather_v(a, half):
            nc.vector.tensor_copy(v[a][:, BANK * half:BANK * (half + 1)],
                                  tab[a][:].bitcast(U32).indirect(idx[:, 32 * half:32 * (half + 1)]))

        def mm(acc, lhs, lhs_scale, rhs, rhs_scale, start, stop):
            nc.tensor.matmul_mx(out=acc, lhsT=lhs, lhsT_scale=lhs_scale, rhs=rhs, rhs_scale=rhs_scale,
                                start=start, stop=stop)

        def v_pass(acc, lhs, lhs_scale, a, half, start, stop):
            cols = slice(BANK * half, BANK * (half + 1))
            mm(acc, lhs, lhs_scale, v[a][:, cols].bitcast(FP8X4), planes[a][:, cols], start, stop)

        gather_v(0, 0)
        gather_v(0, 1)
        w2 = sb("w2", [P, 2, 2 * H], U8)
        nc.vector.tensor_copy(w2[:].rearrange("p a (t m b) -> p a t m b", t=4, b=2),
                              w2_raw[:].rearrange("p a (m t b) -> p a t m b", t=4, b=2))
        gather_v(1, 0)
        gather_v(1, 1)

        w4_first = sb("w4_first", [P, 2, 4, BANK], F32, tag="big0")
        for a in range(2):
            w4_load(0, a, w4_first[:, a])
        w3_s = sb("w3_s", [P, N], U8)
        nc.vector.tensor_copy(w3_s[:].rearrange("p (g t m) -> p g t m", g=2, t=4),
                              w3s_raw[:].rearrange("p (g m t) -> p g t m", g=2, t=4))

        def deal(copy, dst, raw, t0, nt, m0, nm):
            copy(dst.rearrange("p (t m j) -> p m j t", t=nt, j=4)[:, m0:m0 + nm],
                 raw.rearrange("p j (m t) -> p m j t", t=4)[:, m0:m0 + nm, :, t0:t0 + nt])

        def quantise(codes, scales, values):
            nc.vector.quantize_mx(out=codes.bitcast(FP8X4), scales=scales, in_=values)

        w1_bf = [sb("w1_bf%d" % a, [P, 4 * H], BF16) for a in range(2)]
        w1_q = [sb("w1_q%d" % a, [P, H], U32) for a in range(2)]
        w1_s = [sb("w1_s%d" % a, [P, H], U8) for a in range(2)]
        deal(nc.scalar.copy, w1_bf[0][:], w1_raw[0], 0, 4, 0, P)
        quantise(w1_q[0][:], w1_s[0][:], w1_bf[0][:])
        w3_raw = sb("w3_raw", [P, N], I32, tag="mid")
        nc.sync.dma_start(w3_raw[:], w3_words[0].rearrange("p n i -> p (n i)").bitcast(I32))

        units = [(half, t) for half in range(2) for t in range(4)]
        acc = [bank(u, "trend%d" % u) for u in range(8)]
        tg = [sb("tg%d" % half, [P, 4, BANK], F32) for half in range(2)]
        passes = [(4 * half + t, half, t, a) for half in range(2) for a in range(2) for t in range(4)]
        for u, half, t, a in passes:
            if True:
                v_pass(acc[u][:], w2[:, a, 256 * t:256 * (t + 1)].bitcast(FP4X4),
                       planes[a][:, W2_COL + P * t:W2_COL + P * (t + 1)], a, half, a == 0, a == 1)
        for u, (half, t) in enumerate(units[:7]):
            nc.scalar.activation(tg[half][:, t, :], acc[u][:], ACT.Copy, scale=gains[:, t:t + 1])

        deal(nc.vector.tensor_copy, w1_bf[1][:], w1_raw[1], 0, 4, 0, 64)
        deal(nc.vector.tensor_copy, w1_bf[1][:], w1_raw[1], 0, 4, 64, 64)
        for t in range(4):
            quantise(w1_q[1][:, P * t:P * (t + 1)], w1_s[1][:, P * t:P * (t + 1)], w1_bf[1][:, BANK * t:BANK * (t + 1)])

        for u in (7,):
            half, t = units[u]
            nc.vector.tensor_scalar(tg[half][:, t, :], acc[u][:], gains[:, t:t + 1], None, MULT)
        for a in range(2):
            w4_load(1, a, sb("w4_raw1%d" % a, [P, 4, BANK], F32, tag="w1_bf%d" % a)[:])
        y = [at(4 * T * g, "y%d" % g, [P, 4, M], F32)[:] for g in range(2)]
        base_rows = base.rearrange("(g p t) m -> g p t m", g=2, t=4)
        for g in range(2):
            nc.sync.dma_start(y[g], base_rows[g])

        acc = [bank(u, "width%d" % u) for u in range(8)]
        for u, half, t, a in passes:
            if True:
                v_pass(acc[u][:], w1_q[a][:, P * t:P * (t + 1)].bitcast(FP8X4), w1_s[a][:, P * t:P * (t + 1)],
                       a, half, a == 0, a == 1)
        root = [sb("root%d" % half, [P, 4, BANK], F32) for half in range(2)]
        for a0, aw in [(0, 512), (512, 256), (768, 256)]:
            half = a0 // BANK
            cols = slice(a0 % BANK, a0 % BANK + aw)
            for t in range(4):
                nc.scalar.activation(root[half][:, t, cols], acc[4 * half + t][:, cols], ACT.Abs)
            for c0, cw in H_CHUNKS:
                if a0 <= c0 < a0 + aw:
                    part = root[half][:, :, c0 % BANK:c0 % BANK + cw]
                    nc.scalar.activation(part, part, ACT.Sqrt)

        w3 = sb("w3", [P, N], I32)
        nc.vector.tensor_copy(w3[:].rearrange("p (g t m) -> p g m t", g=2, t=4),
                              w3_raw[:].rearrange("p (g m t) -> p g m t", g=2, t=4))
        w4_q = [[sb("w4_q%d%d" % (g, a), [P, BANK], U32) for a in range(2)] for g in range(2)]
        w4_s = [[sb("w4_s%d%d" % (g, a), [P, BANK], U8) for a in range(2)] for g in range(2)]
        w4_bf = {}

        def w4_round(copy, g, a, t0, nt, tag=None):
            if (g, t0) == (1, 2):
                w4_bf[g, a, t0] = w4_bf[g, a, "whole"][:, 2 * BANK:]
            else:
                w4_bf[g, a, "whole"] = sb("w4_bf%d%d%d" % (g, a, t0), [P, 4 * BANK if g else 2 * BANK], BF16, tag=tag)
                w4_bf[g, a, t0] = w4_bf[g, a, "whole"][:, 0:2 * BANK]
            deal(copy, w4_bf[g, a, t0], w4_raw[g, a], t0, nt, 0, P)

        def w4_quantise(g, a, t0, nt):
            cols = slice(P * t0, P * (t0 + nt))
            quantise(w4_q[g][a][:, cols], w4_s[g][a][:, cols], w4_bf[g, a, t0])

        h_bf = sb("h_bf", [P, 4 * S], BF16)
        h_q = sb("h_q", [P, S], U32)
        h_s = sb("h_s", [P, S], U8)

        def h_make(c0, cw):
            nc.vector.tensor_tensor(h_bf[:, 4 * c0:4 * (c0 + cw)].rearrange("p (c i t) -> p c t i", i=4, t=4),
                                    root[c0 // BANK][:, :, c0 % BANK:c0 % BANK + cw].rearrange("p t (c i) -> p c t i", i=4),
                                    tg[c0 // BANK][:, :, c0 % BANK:c0 % BANK + cw].rearrange("p t (c i) -> p c t i", i=4), MULT)

        def h_quantise(c0, cw):
            quantise(h_q[:, c0:c0 + cw], h_s[:, c0:c0 + cw], h_bf[:, 4 * c0:4 * (c0 + cw)])

        w4_round(nc.vector.tensor_copy, 0, 0, 0, 2)
        h_make(*H_CHUNKS[0])
        w4_quantise(0, 0, 0, 2)
        w4_round(nc.vector.tensor_copy, 0, 1, 0, 2)
        h_quantise(*H_CHUNKS[0])
        h_make(*H_CHUNKS[1])
        w4_quantise(0, 1, 0, 2)
        for c in range(1, len(H_CHUNKS)):
            h_quantise(*H_CHUNKS[c])
            if c + 1 < len(H_CHUNKS):
                h_make(*H_CHUNKS[c + 1])

        feat = {}

        def features(s):
            g, t = divmod(s, 4)
            feat[s] = sb("feat%d" % s, [P, S], F32)
            cols = slice(P * t, P * (t + 1))
            n0 = BANK * g + P * t
            for half in range(2):
                out = bank((2 * s + half) % 8, "f%d%d" % (s, half))
                for a in range(2):
                    v_pass(out[:], w4_q[g][a][:, cols].bitcast(FP8X4), w4_s[g][a][:, cols], a, half, a == 0, False)
                pieces = [c for c in H_CHUNKS if c[0] // BANK == half] if s == 0 else [(BANK * half, BANK)]
                for c0, cw in pieces:
                    mm(out[:, c0 - BANK * half:c0 - BANK * half + cw], w3[:, n0:n0 + P].bitcast(FP8X4),
                       w3_s[:, n0:n0 + P], h_q[:, c0:c0 + cw].bitcast(FP8X4),
                       h_s[:, c0:c0 + cw], False, (c0, cw) == pieces[-1])
                copy = nc.vector.tensor_copy if (s, half) == (0, 1) else nc.scalar.copy
                copy(feat[s][:, BANK * half:BANK * (half + 1)], out[:])

        y_rows = out_0.rearrange("(g p t) m -> g p t m", g=2, t=4)
        y_bf = [sb("y_bf%d" % g, [P, 4 * M], BF16) for g in range(2)]
        y_q = [sb("y_q%d" % g, [P, M], I32) for g in range(2)]
        y_s = sb("y_s", [P, 2, M], U8)
        first, second, prod = {}, {}, {}

        def pick(job):
            s, m0, mw = job
            first[job] = ring.tile([P, mw], F32, name="first", tag="first")
            nc.vector.tensor_copy(first[job][:], feat[s][:].indirect(p1[:, m0 // 16:(m0 + mw) // 16]))
            if s in SHARED:
                second[job] = ring.tile([P, mw], F32, name="second", tag="second")
                nc.vector.tensor_copy(second[job][:], feat[s][:].indirect(p2[:, m0 // 16:(m0 + mw) // 16]))

        def multiply(job):
            s, m0, mw = job
            prod[job] = ring.tile([P, mw], F32, name="prod", tag="prod")
            if s in SHARED:
                nc.gpsimd.tensor_tensor(prod[job][:], second[job][:], first[job][:], MULT)
                return
            nc.vector.tensor_tensor(prod[job][:], feat[s][:].indirect(p2[:, m0 // 16:(m0 + mw) // 16]), first[job][:], MULT)

        def add_base(job):
            s, m0, mw = job
            g, t = divmod(s, 4)
            engine = nc.gpsimd if s in SHARED else nc.vector
            engine.tensor_tensor(y[g][:, t, m0:m0 + mw], prod[job][:], y[g][:, t, m0:m0 + mw], ADD)
            nc.sync.dma_start(y_rows[g][:, t, m0:m0 + mw], y[g][:, t, m0:m0 + mw])

        def y_round(copy, g, m0, mw):
            copy(y_bf[g][:, 4 * m0:4 * (m0 + mw)].rearrange("p (c i t) -> p c t i", i=4, t=4),
                 y[g][:, :, m0:m0 + mw].rearrange("p t (c i) -> p c t i", i=4))

        def y_quantise(g, m0, mw):
            quantise(y_q[g][:, m0:m0 + mw], y_s[:, g, m0:m0 + mw], y_bf[g][:, 4 * m0:4 * (m0 + mw)])
            nc.sync.dma_start(out_1[g].rearrange("p m t -> p (m t)").bitcast(I32)[:, m0:m0 + mw], y_q[g][:, m0:m0 + mw])

        jobs = [(s, 0, M) for s in range(7)] + [(7, 0, 256), (7, 256, 128), (7, 384, 128)]
        features(0)
        features(1)
        for a in range(2):
            w4_round(nc.scalar.copy, 0, a, 2, 2, ("tg0", "root0")[a])
        pick(jobs[0])
        for i, job in enumerate(jobs):
            if i == 0:
                for a in range(2):
                    w4_quantise(0, a, 2, 2)
                features(2)
                for a in range(2):
                    w4_round(nc.scalar.copy, 1, a, 0, 2, ("tg1", "root1")[a])
                features(3)
            if i == 1:
                for a in range(2):
                    w4_quantise(1, a, 0, 2)
                features(4)
                for a in range(2):
                    w4_round(nc.scalar.copy, 1, a, 2, 2)
                features(5)
            if i == 3:
                for a in range(2):
                    w4_quantise(1, a, 2, 2)
                features(6)
                features(7)
            if i + 1 < len(jobs):
                pick(jobs[i + 1])
            if i > 0:
                add_base(jobs[i - 1])
            multiply(job)
            if i == 4:
                y_round(nc.scalar.copy, 0, 0, M)
            if i == 6:
                y_quantise(0, 0, M)
            if i == 8:
                y_round(nc.scalar.copy, 1, 0, 256)
        y_round(nc.scalar.copy, 1, 256, 128)
        add_base(jobs[-1])
        y_quantise(1, 0, 256)
        y_round(nc.vector.tensor_copy, 1, 384, 128)
        y_quantise(1, 256, 256)
        for q in range(4):
            queue = nc.scalar if q % 2 else nc.sync
            queue.dma_start(out_2[:, 4 * q:4 * q + 4, :].rearrange("g r m -> r g m").bitcast(I32),
                            y_s[32 * q:32 * q + 4].bitcast(I32))
